import numpy as np
import ml_dtypes


def mxq(x, axis, fmt="e4m3"):
    dtype, down = {"e4m3": (ml_dtypes.float8_e4m3fn, 7), "e5m2": (ml_dtypes.float8_e5m2, 14)}[fmt]
    v = np.moveaxis(np.asarray(x, np.float32).astype(ml_dtypes.bfloat16).astype(np.float64), axis, -1)
    blocks = v.reshape(v.shape[:-1] + (-1, 32))
    amax = np.abs(blocks).max(-1, keepdims=True)
    byte = np.maximum(np.where(amax > 0, np.frexp(amax)[1] - 1 + 127, 0) - down, 1)
    scale = np.exp2(byte - 127.0)
    codes = (blocks / scale).astype(np.float32).astype(dtype).astype(np.float64)
    return np.moveaxis((codes * scale).reshape(v.shape), -1, axis)


WIDE = False


def mx_kscale(k):
    if not WIDE:
        return np.ones(k)
    levels = np.array([10, -10, 5, -5, 0])
    if k % 512:
        return np.exp2(np.random.permutation(np.resize(levels, k // 32))).repeat(32)
    a = np.empty((k // 512, 16))
    for p in range(k // 512):
        a[p, :8] = np.random.permutation(np.resize(levels, 8))
        for g in range(8):
            far = levels[np.abs(levels - a[p, g]) >= 10]
            a[p, g + 8] = far[np.random.randint(len(far))]
    return np.exp2(a.ravel()).repeat(32)


def f64(x):
    return np.asarray(x).astype(np.float64)


def striped(idx):
    return np.tile(idx.reshape(-1, 16).T, (8, 1)).astype(np.uint16)


def unstriped(offs):
    return offs[:16].T.reshape(-1).astype(np.int64)


def pack_weight(w):
    k, n = w.shape
    w = f64(np.asarray(w, np.float32).astype(ml_dtypes.bfloat16)).reshape(k // 32, 32, n)
    amax = np.abs(w).max(1)
    byte = np.clip(np.where(amax > 0, np.frexp(amax)[1] - 1 + 127 - 7, 1), 1, 254)
    scaled = (w * np.exp2(127.0 - byte)[:, None, :]).reshape(k, n).astype(np.float32)
    words = np.ascontiguousarray(scaled.reshape(k // 512, 128, 4, n).transpose(0, 1, 3, 2)).astype(ml_dtypes.float8_e4m3fn).view(np.uint8)
    return words, np.ascontiguousarray(byte.astype(np.uint8).reshape(k // 512, 16, n))


def unpack_weight(words, scales):
    g, p, n, _ = words.shape
    vals = np.ascontiguousarray(words).view(ml_dtypes.float8_e4m3fn).astype(np.float64) * np.repeat(np.exp2(scales.astype(np.float64) - 127.0), 8, axis=1)[..., None]
    return vals.transpose(0, 1, 3, 2).reshape(g * 512, n)


def relu(v):
    return np.maximum(v, 0.0)


K, T, S, N, D = 512, 1024, 512, 128, 3
P = 2 ** 7


def setup_inputs():
    n = np.random.standard_normal
    s = mx_kscale(K)[:, None]
    packed_xT = pack_weight(n((K, T)) * s)
    return {
        "x_words": packed_xT[0],
        "x_scales": packed_xT[1],
        "w1": (n((K, N)) / np.sqrt(K) / s).astype(np.float32),
        "cond": (np.tile(np.random.uniform(0.05, 0.25, (D, 1, S)), (1, P, 1))).astype(np.float32),
        "loss": (np.random.uniform(0.1, 0.5, (N, 1))).astype(np.float32),
        "offs": striped(np.random.permutation(T)[:S]),
        "pos1": striped(np.random.permutation(S)[:S]),
        "pos2": striped(np.random.permutation(S)[:S]),
        "pos3": striped(np.random.permutation(S)[:S]),
    }


def reference(x_words, x_scales, w1, cond, loss, offs, pos1, pos2, pos3):
    xq = unpack_weight(x_words, x_scales)[:, unstriped(offs)]
    y = mxq(f64(w1), 0, "e4m3").T @ xq
    tm0 = relu(y - 0.6) - relu(-1.0 * y)
    ent = y + (tm0[:, unstriped(pos1)] - tm0) * f64(cond)[0, :1] + (tm0[:, unstriped(pos2)] - tm0) * f64(cond)[1, :1] + (tm0[:, unstriped(pos3)] - tm0) * f64(cond)[2, :1]
    return 1.666667 * (relu(ent) - relu(ent - 0.6)) - (f64(loss) * ((relu(ent - 0.6) - relu(-1.0 * ent)) ** 2))

@@ -1,0 +1,169 @@
+from contextlib import ExitStack
+
+import concourse.mybir as mybir
+from concourse.masks import make_identity
+
+F32 = mybir.dt.float32
+BF16 = mybir.dt.bfloat16
+I32 = mybir.dt.int32
+U32 = mybir.dt.uint32
+U16 = mybir.dt.uint16
+U8 = mybir.dt.uint8
+FP8X4 = mybir.dt.float8_e4m3fn_x4
+ALU = mybir.AluOpType
+ACT = mybir.ActivationFunctionType
+
+P = 128
+K, T, S, D = 512, 1024, 512, 3
+PACK = 4
+LATENT = 0.6
+SHARE = 1.666667
+PIECES = ((0, 256), (256, 384), (384, 512))
+HALF = 256
+BLOCKS = S // P
+
+FLOPS = 2 * K * P * S
+
+
+def tile_picked_ystefn_melt_p_kernel(
+    tc, x_words, x_scales, w1, cond, loss, offs, pos1, pos2, pos3, out
+):
+    nc = tc.nc
+    with ExitStack() as ctx:
+        lists = ctx.enter_context(tc.tile_pool(name="lists", bufs=1))
+        sb = ctx.enter_context(tc.tile_pool(name="sb", bufs=1))
+        ps = ctx.enter_context(tc.psum_pool(name="ps", bufs=1))
+
+        picked = lists.tile([P, S // 16], U16, name="picked")
+        nbr = [lists.tile([P, S // 16], U16, name="nbr%d" % d) for d in range(D)]
+
+        x_scale_rows = sb.tile([P, T], U8, name="x_scale_rows")
+        nc.gpsimd.memset(x_scale_rows[:].bitcast(I32), 0)
+        cond_rows = sb.tile([P, D, P], F32, name="cond_rows")
+        nc.gpsimd.memset(cond_rows[:], 0.0)
+        ident = sb.tile([P, P], F32, name="ident")
+        make_identity(nc, ident[:])
+
+        nc.sync.dma_start(picked[:], offs)
+        w_raw = sb.tile([P, PACK, P], F32, name="w_raw")
+        nc.sync.dma_start(w_raw[:], w1.rearrange("(p j) m -> p j m", j=PACK))
+        for q in range(4):
+            nc.sync.dma_start(
+                x_scale_rows[32 * q : 32 * q + 4, :].bitcast(I32),
+                x_scales[0, 4 * q : 4 * q + 4, :].bitcast(I32),
+            )
+        x_word_cols = sb.tile([P, T], U32, name="x_word_cols")
+        nc.sync.dma_start(
+            x_word_cols[:].bitcast(I32),
+            x_words[0].rearrange("p n t -> p (n t)").bitcast(I32),
+        )
+        nc.sync.dma_start(
+            cond_rows[0:BLOCKS, :, :], cond[:, 0, :].rearrange("d (b c) -> b d c", b=BLOCKS)
+        )
+        cond_sb = [sb.tile([P, S], F32, name="cond%d" % d) for d in range(D)]
+        for d, pos in enumerate((pos1, pos2, pos3)):
+            nc.sync.dma_start(nbr[d][:], pos)
+            nc.sync.dma_start(cond_sb[d][:], cond[d])
+        loss_sb = sb.tile([P, 1], F32, name="loss_sb")
+        nc.sync.dma_start(loss_sb[:], loss)
+
+        scale_g = sb.tile([P, S], U8, name="scale_g", align_bytes=64)
+        nc.vector.tensor_copy(scale_g[:], x_scale_rows[:].indirect(picked[:]))
+
+        w_grouped = sb.tile([P, P, PACK], BF16, name="w_grouped", align_bytes=64)
+        nc.scalar.activation(w_grouped[:], w_raw[:].rearrange("p j m -> p m j"), ACT.Copy)
+        w_codes = sb.tile([P, P], U32, name="w_codes", align_bytes=64)
+        w_scales = sb.tile([P, P], U8, name="w_scales", align_bytes=64)
+        nc.vector.quantize_mx(
+            out=w_codes[:].bitcast(FP8X4),
+            scales=w_scales[:],
+            in_=w_grouped[:].rearrange("p m j -> p (m j)"),
+        )
+
+        csum_ps = ps.tile([P, P], F32, name="csum_ps", tag="flip1")
+        for d in range(D):
+            nc.tensor.matmul(csum_ps[:], cond_rows[:, d, :], ident[:], start=d == 0, stop=d == D - 1, is_transpose=True)
+        outflow = sb.tile([P, BLOCKS], F32, name="outflow")
+        nc.scalar.activation(outflow[:], csum_ps[:, 0:BLOCKS], ACT.Copy, scale=-SHARE)
+
+        temp = sb.tile([P, S], F32, name="temp")
+        y_ps = []
+        for i, (a, b) in enumerate(PIECES):
+            word_g = sb.tile([P, b - a], U32, name="word_g%d" % i, align_bytes=64)
+            nc.vector.tensor_copy(word_g[:], x_word_cols[:].indirect(picked[:, a // 16 : b // 16]))
+            y = ps.tile([P, b - a], F32, name="y%d" % i)
+            nc.tensor.matmul_mx(
+                out=y[:],
+                lhsT=w_codes[:].bitcast(FP8X4),
+                lhsT_scale=w_scales[:],
+                rhs=word_g[:].bitcast(FP8X4),
+                rhs_scale=scale_g[:, a:b],
+                start=True,
+                stop=True,
+            )
+            y_ps.append(y)
+        for i, (a, b) in enumerate(PIECES):
+            above = sb.tile([P, b - a], F32, name="above%d" % i)
+            nc.scalar.activation(above[:], y_ps[i][:], ACT.Relu, bias=-LATENT)
+            nc.vector.scalar_tensor_tensor(temp[:, a:b], y_ps[i][:], 0.0, above[:], ALU.min, ALU.add)
+        y_sb = sb.tile([P, S], F32, name="y_sb")
+        for i, (a, b) in enumerate(PIECES):
+            nc.scalar.copy(y_sb[:, a:b], y_ps[i][:])
+
+        temp_t = ps.tile([P, BLOCKS, P], F32, name="temp_t")
+        for b in range(BLOCKS):
+            nc.tensor.transpose(temp_t[:, b, :], temp[:, P * b : P * (b + 1)], ident[:])
+        own_t = sb.tile([P, BLOCKS, P], F32, name="own_t")
+        for b in range(BLOCKS):
+            nc.scalar.activation(own_t[:, b, :], temp_t[:, b, :], ACT.Copy, scale=outflow[:, b : b + 1])
+        loss_k = sb.tile([P, 1], F32, name="loss_k")
+        nc.scalar.activation(loss_k[:], loss_sb[:], ACT.Copy, scale=-1.0 / (SHARE * SHARE))
+
+        inflow = [[sb.tile([P, HALF], F32, name="inflow%d_%d" % (d, h)) for h in range(2)] for d in range(D)]
+        for d in range(D):
+            for h in range(2):
+                nc.vector.tensor_tensor(
+                    inflow[d][h][:],
+                    temp[:].indirect(nbr[d][:, 16 * h : 16 * (h + 1)]),
+                    cond_sb[d][:, HALF * h : HALF * (h + 1)],
+                    ALU.mult,
+                )
+        partial = []
+        for h in range(2):
+            sum_t = ps.tile([P, 2, P], F32, name="sum_t%d" % h, tag="flip%d" % h)
+            terms = [y_sb[:, HALF * h : HALF * (h + 1)], inflow[0][h][:], inflow[1][h][:]]
+            for n, term in enumerate(terms):
+                for b in range(2):
+                    nc.tensor.matmul(
+                        sum_t[:, b, :], term[:, P * b : P * (b + 1)], ident[:],
+                        start=n == 0 and b == 0, stop=n == 2 and b == 1, is_transpose=True,
+                    )
+            sum_sb = sb.tile([P, 2, P], F32, name="sum_sb%d" % h)
+            nc.scalar.activation(sum_sb[:], sum_t[:], ACT.Copy, scale=SHARE)
+            part = ps.tile([P, 2, P], F32, name="part%d" % h)
+            terms = [own_t[:, 2 * h : 2 * h + 2, :], sum_sb[:]]
+            for n, term in enumerate(terms):
+                for b in range(2):
+                    nc.tensor.matmul(
+                        part[:, b, :], term[:, b, :], ident[:],
+                        start=n == 0 and b == 0, stop=n == 1 and b == 1, is_transpose=True,
+                    )
+            partial.append(part)
+
+        ent = [sb.tile([P, HALF], F32, name="ent%d" % h) for h in range(2)]
+        melt = [sb.tile([P, HALF], F32, name="melt%d" % h) for h in range(2)]
+        heat = [sb.tile([P, HALF], F32, name="heat%d" % h) for h in range(2)]
+        heat2 = [sb.tile([P, HALF], F32, name="heat2_%d" % h) for h in range(2)]
+        res = [sb.tile([P, HALF], F32, name="res%d" % h) for h in range(2)]
+        for h in range(2):
+            nc.vector.scalar_tensor_tensor(
+                ent[h][:], inflow[2][h][:], SHARE, partial[h][:].rearrange("p b c -> p (b c)"), ALU.mult, ALU.add
+            )
+        for h in range(2):
+            nc.vector.tensor_scalar(melt[h][:], ent[h][:], 0.0, SHARE * LATENT, ALU.max, ALU.min)
+        for h in range(2):
+            nc.vector.tensor_tensor(heat[h][:], ent[h][:], melt[h][:], ALU.subtract)
+            nc.scalar.activation(heat2[h][:], heat[h][:], ACT.Square)
+        for h in range(2):
+            nc.vector.scalar_tensor_tensor(res[h][:], heat2[h][:], loss_k[:, 0:1], melt[h][:], ALU.mult, ALU.add)
+            nc.sync.dma_start(out[:, HALF * h : HALF * (h + 1)], res[h][:])

@@ -80,18 +80,12 @@ def tile_picked_ystefn_melt_p_kernel(
             in_=w_grouped[:].rearrange("p m j -> p (m j)"),
         )
 
-        csum_ps = ps.tile([P, P], F32, name="csum_ps", tag="flip1")
-        for d in range(D):
-            nc.tensor.matmul(csum_ps[:], cond_rows[:, d, :], ident[:], start=d == 0, stop=d == D - 1, is_transpose=True)
-        outflow = sb.tile([P, BLOCKS], F32, name="outflow")
-        nc.scalar.activation(outflow[:], csum_ps[:, 0:BLOCKS], ACT.Copy, scale=-SHARE)
-
         temp = sb.tile([P, S], F32, name="temp")
         y_ps = []
         for i, (a, b) in enumerate(PIECES):
             word_g = sb.tile([P, b - a], U32, name="word_g%d" % i, align_bytes=64)
             nc.vector.tensor_copy(word_g[:], x_word_cols[:].indirect(picked[:, a // 16 : b // 16]))
-            y = ps.tile([P, b - a], F32, name="y%d" % i)
+            y = ps.tile([P, b - a], F32, name="y%d" % i, tag="first%d" % i)
             nc.tensor.matmul_mx(
                 out=y[:],
                 lhsT=w_codes[:].bitcast(FP8X4),
@@ -102,68 +96,88 @@ def tile_picked_ystefn_melt_p_kernel(
                 stop=True,
             )
             y_ps.append(y)
+        latent = sb.tile([P, S], F32, name="latent")
         for i, (a, b) in enumerate(PIECES):
-            above = sb.tile([P, b - a], F32, name="above%d" % i)
-            nc.scalar.activation(above[:], y_ps[i][:], ACT.Relu, bias=-LATENT)
-            nc.vector.scalar_tensor_tensor(temp[:, a:b], y_ps[i][:], 0.0, above[:], ALU.min, ALU.add)
-        y_sb = sb.tile([P, S], F32, name="y_sb")
-        for i, (a, b) in enumerate(PIECES):
-            nc.scalar.copy(y_sb[:, a:b], y_ps[i][:])
+            nc.vector.tensor_scalar(latent[:, a:b], y_ps[i][:], 0.0, LATENT, ALU.max, ALU.min)
+            nc.vector.tensor_tensor(temp[:, a:b], y_ps[i][:], latent[:, a:b], ALU.subtract)
 
-        temp_t = ps.tile([P, BLOCKS, P], F32, name="temp_t")
-        for b in range(BLOCKS):
-            nc.tensor.transpose(temp_t[:, b, :], temp[:, P * b : P * (b + 1)], ident[:])
-        own_t = sb.tile([P, BLOCKS, P], F32, name="own_t")
-        for b in range(BLOCKS):
-            nc.scalar.activation(own_t[:, b, :], temp_t[:, b, :], ACT.Copy, scale=outflow[:, b : b + 1])
+        csum_ps = ps.tile([P, P], F32, name="csum_ps", tag="csum")
+        for d in range(D):
+            nc.tensor.matmul(csum_ps[:], cond_rows[:, d, :], ident[:], start=d == 0, stop=d == D - 1, is_transpose=True)
+        outflow = sb.tile([P, BLOCKS], F32, name="outflow")
+        nc.scalar.activation(outflow[:], csum_ps[:, 0:BLOCKS], ACT.Copy, scale=-SHARE, bias=SHARE)
+
+        own_t = sb.tile([P, S], F32, name="own_t")
+        partial = []
+        for i, (a, b) in enumerate(PIECES):
+            temp_t = ps.tile([P, b - a], F32, name="temp_t%d" % i, tag="second%d" % i)
+            for c in range(a, b, P):
+                nc.tensor.transpose(temp_t[:, c - a : c - a + P], temp[:, c : c + P], ident[:])
+            for c in range(a, b, P):
+                nc.scalar.activation(
+                    own_t[:, c : c + P], temp_t[:, c - a : c - a + P], ACT.Copy, scale=outflow[:, c // P : c // P + 1]
+                )
+            part = ps.tile([P, b - a], F32, name="part%d" % i, tag="second%d" % i)
+            for c in range(a, b, P):
+                nc.tensor.matmul(
+                    part[:, c - a : c - a + P], own_t[:, c : c + P], ident[:], start=c == a, stop=False, is_transpose=True
+                )
+            partial.append(part)
+
         loss_k = sb.tile([P, 1], F32, name="loss_k")
         nc.scalar.activation(loss_k[:], loss_sb[:], ACT.Copy, scale=-1.0 / (SHARE * SHARE))
 
-        inflow = [[sb.tile([P, HALF], F32, name="inflow%d_%d" % (d, h)) for h in range(2)] for d in range(D)]
-        for d in range(D):
-            for h in range(2):
-                nc.vector.tensor_tensor(
-                    inflow[d][h][:],
-                    temp[:].indirect(nbr[d][:, 16 * h : 16 * (h + 1)]),
-                    cond_sb[d][:, HALF * h : HALF * (h + 1)],
-                    ALU.mult,
+        def fetch(d, a, b):
+            flow = sb.tile([P, b - a], F32, name="inflow%d_%d" % (d, a))
+            nc.vector.tensor_tensor(
+                flow[:], temp[:].indirect(nbr[d][:, a // 16 : b // 16]), cond_sb[d][:, a:b], ALU.mult
+            )
+            return flow
+
+        flow0 = [fetch(0, HALF * h, HALF * (h + 1)) for h in range(2)]
+        flow1 = [fetch(1, a, b) for a, b in PIECES]
+        flow2 = [fetch(2, HALF * h, HALF * (h + 1)) for h in range(2)]
+        sum_t = [ps.tile([P, b - a], F32, name="sum_t%d" % i, tag="first%d" % i) for i, (a, b) in enumerate(PIECES)]
+
+        def add_turned(acc, term, first, last):
+            width = term.shape[1]
+            for c in range(0, width, P):
+                nc.tensor.matmul(
+                    acc[:, c : c + P], term[:, c : c + P], ident[:],
+                    start=first and c == 0, stop=last and c == width - P, is_transpose=True,
                 )
-        partial = []
-        for h in range(2):
-            sum_t = ps.tile([P, 2, P], F32, name="sum_t%d" % h, tag="flip%d" % h)
-            terms = [y_sb[:, HALF * h : HALF * (h + 1)], inflow[0][h][:], inflow[1][h][:]]
-            for n, term in enumerate(terms):
-                for b in range(2):
-                    nc.tensor.matmul(
-                        sum_t[:, b, :], term[:, P * b : P * (b + 1)], ident[:],
-                        start=n == 0 and b == 0, stop=n == 2 and b == 1, is_transpose=True,
-                    )
-            sum_sb = sb.tile([P, 2, P], F32, name="sum_sb%d" % h)
-            nc.scalar.activation(sum_sb[:], sum_t[:], ACT.Copy, scale=SHARE)
-            part = ps.tile([P, 2, P], F32, name="part%d" % h)
-            terms = [own_t[:, 2 * h : 2 * h + 2, :], sum_sb[:]]
-            for n, term in enumerate(terms):
-                for b in range(2):
-                    nc.tensor.matmul(
-                        part[:, b, :], term[:, b, :], ident[:],
-                        start=n == 0 and b == 0, stop=n == 1 and b == 1, is_transpose=True,
-                    )
-            partial.append(part)
+
+        for i, (a, b) in enumerate(PIECES):
+            add_turned(sum_t[i], latent[:, a:b], True, False)
+        for i, (a, b) in enumerate(PIECES):
+            h = a // HALF
+            add_turned(sum_t[i], flow0[h][:, a - HALF * h : b - HALF * h], False, False)
+        for i, (a, b) in enumerate(PIECES):
+            add_turned(sum_t[i], flow1[i][:], False, True)
+            sum_sb = sb.tile([P, b - a], F32, name="sum_sb%d" % i)
+            nc.scalar.activation(sum_sb[:], sum_t[i][:], ACT.Copy, scale=SHARE)
+            add_turned(partial[i], sum_sb[:], False, True)
 
         ent = [sb.tile([P, HALF], F32, name="ent%d" % h) for h in range(2)]
         melt = [sb.tile([P, HALF], F32, name="melt%d" % h) for h in range(2)]
-        heat = [sb.tile([P, HALF], F32, name="heat%d" % h) for h in range(2)]
-        heat2 = [sb.tile([P, HALF], F32, name="heat2_%d" % h) for h in range(2)]
+        hot = [sb.tile([P, HALF], F32, name="hot%d" % h) for h in range(2)]
+        hot2 = [sb.tile([P, HALF], F32, name="hot2_%d" % h) for h in range(2)]
+        cold2 = [sb.tile([P, HALF], F32, name="cold2_%d" % h) for h in range(2)]
+        rest = [sb.tile([P, HALF], F32, name="rest%d" % h) for h in range(2)]
         res = [sb.tile([P, HALF], F32, name="res%d" % h) for h in range(2)]
+        for i, (a, b) in enumerate(PIECES):
+            h = a // HALF
+            cols = slice(a - HALF * h, b - HALF * h)
+            nc.vector.scalar_tensor_tensor(ent[h][:, cols], flow2[h][:, cols], SHARE, partial[i][:], ALU.mult, ALU.add)
         for h in range(2):
-            nc.vector.scalar_tensor_tensor(
-                ent[h][:], inflow[2][h][:], SHARE, partial[h][:].rearrange("p b c -> p (b c)"), ALU.mult, ALU.add
-            )
+            nc.scalar.activation(hot[h][:], ent[h][:], ACT.Relu, bias=-SHARE * LATENT)
         for h in range(2):
+            nc.scalar.activation(hot2[h][:], hot[h][:], ACT.Square)
+        for h in range(2):
+            nc.vector.scalar_tensor_tensor(cold2[h][:], ent[h][:], 0.0, ent[h][:], ALU.min, ALU.mult)
             nc.vector.tensor_scalar(melt[h][:], ent[h][:], 0.0, SHARE * LATENT, ALU.max, ALU.min)
         for h in range(2):
-            nc.vector.tensor_tensor(heat[h][:], ent[h][:], melt[h][:], ALU.subtract)
-            nc.scalar.activation(heat2[h][:], heat[h][:], ACT.Square)
+            nc.vector.scalar_tensor_tensor(rest[h][:], cold2[h][:], loss_k[:, 0:1], melt[h][:], ALU.mult, ALU.add)
         for h in range(2):
-            nc.vector.scalar_tensor_tensor(res[h][:], heat2[h][:], loss_k[:, 0:1], melt[h][:], ALU.mult, ALU.add)
+            nc.vector.scalar_tensor_tensor(res[h][:], hot2[h][:], loss_k[:, 0:1], rest[h][:], ALU.mult, ALU.add)
             nc.sync.dma_start(out[:, HALF * h : HALF * (h + 1)], res[h][:])

from contextlib import ExitStack

import concourse.mybir as mybir
from concourse.masks import make_identity

F32 = mybir.dt.float32
BF16 = mybir.dt.bfloat16
I32 = mybir.dt.int32
U32 = mybir.dt.uint32
U16 = mybir.dt.uint16
U8 = mybir.dt.uint8
FP8X4 = mybir.dt.float8_e4m3fn_x4
ALU = mybir.AluOpType
ACT = mybir.ActivationFunctionType

P = 128
K, T, S, D = 512, 1024, 512, 3
PACK = 4
LATENT = 0.6
SHARE = 1.666667
PIECES = ((0, 256), (256, 384), (384, 512))
HALF = 256
BLOCKS = S // P

FLOPS = 2 * K * P * S


def tile_picked_ystefn_melt_p_kernel(
    tc, x_words, x_scales, w1, cond, loss, offs, pos1, pos2, pos3, out
):
    nc = tc.nc
    with ExitStack() as ctx:
        lists = ctx.enter_context(tc.tile_pool(name="lists", bufs=1))
        sb = ctx.enter_context(tc.tile_pool(name="sb", bufs=1))
        ps = ctx.enter_context(tc.psum_pool(name="ps", bufs=1))

        picked = lists.tile([P, S // 16], U16, name="picked")
        nbr = [lists.tile([P, S // 16], U16, name="nbr%d" % d) for d in range(D)]

        x_scale_rows = sb.tile([P, T], U8, name="x_scale_rows")
        nc.gpsimd.memset(x_scale_rows[:].bitcast(I32), 0)
        cond_rows = sb.tile([P, D, P], F32, name="cond_rows")
        nc.gpsimd.memset(cond_rows[:], 0.0)
        ident = sb.tile([P, P], F32, name="ident")
        make_identity(nc, ident[:])

        nc.sync.dma_start(picked[:], offs)
        w_raw = sb.tile([P, PACK, P], F32, name="w_raw")
        nc.sync.dma_start(w_raw[:], w1.rearrange("(p j) m -> p j m", j=PACK))
        for q in range(4):
            nc.sync.dma_start(
                x_scale_rows[32 * q : 32 * q + 4, :].bitcast(I32),
                x_scales[0, 4 * q : 4 * q + 4, :].bitcast(I32),
            )
        x_word_cols = sb.tile([P, T], U32, name="x_word_cols")
        nc.sync.dma_start(
            x_word_cols[:].bitcast(I32),
            x_words[0].rearrange("p n t -> p (n t)").bitcast(I32),
        )
        nc.sync.dma_start(
            cond_rows[0:BLOCKS, :, :], cond[:, 0, :].rearrange("d (b c) -> b d c", b=BLOCKS)
        )
        cond_sb = [sb.tile([P, S], F32, name="cond%d" % d) for d in range(D)]
        for d, pos in enumerate((pos1, pos2, pos3)):
            nc.sync.dma_start(nbr[d][:], pos)
            nc.sync.dma_start(cond_sb[d][:], cond[d])
        loss_sb = sb.tile([P, 1], F32, name="loss_sb")
        nc.sync.dma_start(loss_sb[:], loss)

        scale_g = sb.tile([P, S], U8, name="scale_g", align_bytes=64)
        nc.vector.tensor_copy(scale_g[:], x_scale_rows[:].indirect(picked[:]))

        w_grouped = sb.tile([P, P, PACK], BF16, name="w_grouped", align_bytes=64)
        nc.scalar.activation(w_grouped[:], w_raw[:].rearrange("p j m -> p m j"), ACT.Copy)
        w_codes = sb.tile([P, P], U32, name="w_codes", align_bytes=64)
        w_scales = sb.tile([P, P], U8, name="w_scales", align_bytes=64)
        nc.vector.quantize_mx(
            out=w_codes[:].bitcast(FP8X4),
            scales=w_scales[:],
            in_=w_grouped[:].rearrange("p m j -> p (m j)"),
        )

        temp = sb.tile([P, S], F32, name="temp")
        y_ps = []
        for i, (a, b) in enumerate(PIECES):
            word_g = sb.tile([P, b - a], U32, name="word_g%d" % i, align_bytes=64)
            nc.vector.tensor_copy(word_g[:], x_word_cols[:].indirect(picked[:, a // 16 : b // 16]))
            y = ps.tile([P, b - a], F32, name="y%d" % i, tag="first%d" % i)
            nc.tensor.matmul_mx(
                out=y[:],
                lhsT=w_codes[:].bitcast(FP8X4),
                lhsT_scale=w_scales[:],
                rhs=word_g[:].bitcast(FP8X4),
                rhs_scale=scale_g[:, a:b],
                start=True,
                stop=True,
            )
            y_ps.append(y)
        latent = sb.tile([P, S], F32, name="latent")
        for i, (a, b) in enumerate(PIECES):
            nc.vector.tensor_scalar(latent[:, a:b], y_ps[i][:], 0.0, LATENT, ALU.max, ALU.min)
            nc.vector.tensor_tensor(temp[:, a:b], y_ps[i][:], latent[:, a:b], ALU.subtract)

        csum_ps = ps.tile([P, P], F32, name="csum_ps", tag="csum")
        for d in range(D):
            nc.tensor.matmul(csum_ps[:], cond_rows[:, d, :], ident[:], start=d == 0, stop=d == D - 1, is_transpose=True)
        outflow = sb.tile([P, BLOCKS], F32, name="outflow")
        nc.scalar.activation(outflow[:], csum_ps[:, 0:BLOCKS], ACT.Copy, scale=-SHARE, bias=SHARE)

        own_t = sb.tile([P, S], F32, name="own_t")
        partial = []
        for i, (a, b) in enumerate(PIECES):
            temp_t = ps.tile([P, b - a], F32, name="temp_t%d" % i, tag="second%d" % i)
            for c in range(a, b, P):
                nc.tensor.transpose(temp_t[:, c - a : c - a + P], temp[:, c : c + P], ident[:])
            for c in range(a, b, P):
                nc.scalar.activation(
                    own_t[:, c : c + P], temp_t[:, c - a : c - a + P], ACT.Copy, scale=outflow[:, c // P : c // P + 1]
                )
            part = ps.tile([P, b - a], F32, name="part%d" % i, tag="second%d" % i)
            for c in range(a, b, P):
                nc.tensor.matmul(
                    part[:, c - a : c - a + P], own_t[:, c : c + P], ident[:], start=c == a, stop=False, is_transpose=True
                )
            partial.append(part)

        loss_k = sb.tile([P, 1], F32, name="loss_k")
        nc.scalar.activation(loss_k[:], loss_sb[:], ACT.Copy, scale=-1.0 / (SHARE * SHARE))

        def fetch(d, a, b):
            flow = sb.tile([P, b - a], F32, name="inflow%d_%d" % (d, a))
            nc.vector.tensor_tensor(
                flow[:], temp[:].indirect(nbr[d][:, a // 16 : b // 16]), cond_sb[d][:, a:b], ALU.mult
            )
            return flow

        flow0 = [fetch(0, HALF * h, HALF * (h + 1)) for h in range(2)]
        flow1 = [fetch(1, a, b) for a, b in PIECES]
        flow2 = [fetch(2, HALF * h, HALF * (h + 1)) for h in range(2)]
        sum_t = [ps.tile([P, b - a], F32, name="sum_t%d" % i, tag="first%d" % i) for i, (a, b) in enumerate(PIECES)]

        def add_turned(acc, term, first, last):
            width = term.shape[1]
            for c in range(0, width, P):
                nc.tensor.matmul(
                    acc[:, c : c + P], term[:, c : c + P], ident[:],
                    start=first and c == 0, stop=last and c == width - P, is_transpose=True,
                )

        for i, (a, b) in enumerate(PIECES):
            add_turned(sum_t[i], latent[:, a:b], True, False)
        for i, (a, b) in enumerate(PIECES):
            h = a // HALF
            add_turned(sum_t[i], flow0[h][:, a - HALF * h : b - HALF * h], False, False)
        for i, (a, b) in enumerate(PIECES):
            add_turned(sum_t[i], flow1[i][:], False, True)
            sum_sb = sb.tile([P, b - a], F32, name="sum_sb%d" % i)
            nc.scalar.activation(sum_sb[:], sum_t[i][:], ACT.Copy, scale=SHARE)
            add_turned(partial[i], sum_sb[:], False, True)

        ent = [sb.tile([P, HALF], F32, name="ent%d" % h) for h in range(2)]
        melt = [sb.tile([P, HALF], F32, name="melt%d" % h) for h in range(2)]
        hot = [sb.tile([P, HALF], F32, name="hot%d" % h) for h in range(2)]
        hot2 = [sb.tile([P, HALF], F32, name="hot2_%d" % h) for h in range(2)]
        cold2 = [sb.tile([P, HALF], F32, name="cold2_%d" % h) for h in range(2)]
        rest = [sb.tile([P, HALF], F32, name="rest%d" % h) for h in range(2)]
        res = [sb.tile([P, HALF], F32, name="res%d" % h) for h in range(2)]
        for i, (a, b) in enumerate(PIECES):
            h = a // HALF
            cols = slice(a - HALF * h, b - HALF * h)
            nc.vector.scalar_tensor_tensor(ent[h][:, cols], flow2[h][:, cols], SHARE, partial[i][:], ALU.mult, ALU.add)
        for h in range(2):
            nc.scalar.activation(hot[h][:], ent[h][:], ACT.Relu, bias=-SHARE * LATENT)
        for h in range(2):
            nc.scalar.activation(hot2[h][:], hot[h][:], ACT.Square)
        for h in range(2):
            nc.vector.scalar_tensor_tensor(cold2[h][:], ent[h][:], 0.0, ent[h][:], ALU.min, ALU.mult)
            nc.vector.tensor_scalar(melt[h][:], ent[h][:], 0.0, SHARE * LATENT, ALU.max, ALU.min)
        for h in range(2):
            nc.vector.scalar_tensor_tensor(rest[h][:], cold2[h][:], loss_k[:, 0:1], melt[h][:], ALU.mult, ALU.add)
        for h in range(2):
            nc.vector.scalar_tensor_tensor(res[h][:], hot2[h][:], loss_k[:, 0:1], rest[h][:], ALU.mult, ALU.add)
            nc.sync.dma_start(out[:, HALF * h : HALF * (h + 1)], res[h][:])
